import numpy as np, ml_dtypes
CORES = [1,2,5,7,57,58,61,63,73,74,77,79]
N = 12
KT, C = 4, 128
def setup_inputs(rng):
    return {"x": rng.standard_normal((N, 128, KT * C), dtype=np.float32).astype(ml_dtypes.bfloat16)}
def setup_inputs_big(rng):
    d = setup_inputs(rng)
    for k in ("x",): d[k] = (d[k].astype(np.float32) * 1024.0).astype(d[k].dtype)
    return d
def setup_inputs_small(rng):
    d = setup_inputs(rng)
    for k in ("x",): d[k] = (d[k].astype(np.float32) * (1 / 1024.0)).astype(d[k].dtype)
    return d
def setup_inputs_apart(rng):
    d = setup_inputs(rng)
    f = (10.0 ** rng.permutation(np.linspace(-1.5, 1.5, N))).astype(np.float32).reshape(N, 1, 1)
    for k in ("x",): d[k] = (d[k].astype(np.float32) * f).astype(d[k].dtype)
    return d
def reference(x):
    X = x.astype(np.float64)
    y = np.full((N, C, N * C), np.nan)
    for r in range(N):
        for i in range(N):
            s = i
            if s != r: y[r][:, C * i:C * i + C] = sum(X[r][:, C * t:C * t + C].T @ X[s][:, C * t:C * t + C] for t in range(KT))
    return {"y": y.astype(ml_dtypes.bfloat16 if x.dtype != np.float64 else np.float64)}

@@ -1,0 +1,259 @@
+from concourse.bass import DstId, RemoteDMATransfer
+
+KT, C = 4, 128
+W = KT * C
+NSLOT = 2
+NOTH = 3
+
+SCRATCH = {
+    "xall": ("sbuf", [128, 4 * W], "bfloat16"),
+    "xrem": ("sbuf", [128, NSLOT * W], "bfloat16"),
+    "gsend": ("sbuf", [128, NSLOT * NOTH * C], "bfloat16"),
+    "ybuf": ("sbuf", [128, 12 * C], "bfloat16"),
+    "pchip": ("psum", [128, 512], "float32"),
+    "poth0": ("psum", [128, 512], "float32"),
+    "poth1": ("psum", [128, 512], "float32"),
+    "pmine0": ("psum", [128, 512], "float32"),
+    "pmine1": ("psum", [128, 512], "float32"),
+}
+SEMAPHORES = (["ld", "snt", "mchip"]
+              + ["ax%d" % j for j in range(4)]
+              + ["rx%d" % k for k in range(NSLOT)]
+              + ["moth%d" % k for k in range(NSLOT)] + ["mmine%d" % k for k in range(NSLOT)]
+              + ["gready%d" % k for k in range(NSLOT)]
+              + ["yl%d" % i for i in range(3)] + ["yr%d" % i for i in range(3)] + ["st%d" % i for i in range(3)])
+
+
+def _bits(mask):
+    return [i for i in range(mask.bit_length()) if (mask >> i) & 1]
+
+
+def _mk(engs):
+    m = 0
+    for e in engs:
+        m |= 1 << e
+    return m
+
+
+def _split(engs, n):
+    per = 1
+    while per * 2 * n <= len(engs):
+        per *= 2
+    return [engs[i * per:(i + 1) * per] for i in range(n)]
+
+
+def _plan(T, topo):
+    cores = list(T.cores)
+    chips = []
+    for c in cores:
+        if topo.chip(c) not in chips:
+            chips.append(topo.chip(c))
+    mem = {ch: [c for c in cores if topo.chip(c) == ch] for ch in chips}
+
+    owned = {c: [] for c in cores}
+    owner = {}
+    for B in chips:
+        for d in sorted(set(topo.die(o) for o in mem[B])):
+            R = [o for o in mem[B] if topo.die(o) == d]
+            srcs = [a for a in cores if topo.chip(a) != B and topo.die(a) == d]
+            srcs.sort(key=lambda a: 0 if topo.may_write(a, R[0]) else 1)
+            for i, a in enumerate(srcs):
+                o = R[i % len(R)]
+                owner[(a, B)] = (o, len(owned[o]))
+                owned[o].append(a)
+
+    def relay(a, dst):
+        if topo.may_write(a, dst):
+            return None
+        cand = [p for p in mem[topo.chip(a)] if p != a and topo.may_write(p, dst)]
+        cand.sort(key=lambda p: 0 if topo.die(p) == topo.die(a) else 1)
+        return cand[0]
+
+    calls = {c: [] for c in cores}
+    expect = {}
+
+    def add(dst, sem, n):
+        expect[(dst, sem)] = expect.get((dst, sem), 0) + n
+
+    relays = {}
+    for c in cores:
+        A = topo.chip(c)
+        j = mem[A].index(c)
+        others = [p for p in mem[A] if p != c]
+        on = topo.mask(c, others[0])
+        off = on
+        for a in cores:
+            if topo.chip(a) != A:
+                off &= topo.mask(c, a)
+        lo, hi = _bits(on & off), _bits(on & ~off)
+        cross, via = [], None
+        for B in chips:
+            if B != A:
+                o, k = owner[(c, B)]
+                p = relay(c, o)
+                if p is None:
+                    cross.append((o, k))
+                else:
+                    via = p
+                    relays.setdefault(p, {}).setdefault(c, []).append((o, k))
+        rest = others
+        if via is not None:
+            calls[c].append([("x", j, [via], None, hi)])
+            rest = [p for p in others if p != via]
+        trs = []
+        if cross:
+            for (o, k), e in zip(cross, _split(lo, len(cross))):
+                trs.append(("r", j, [o], k, e))
+            trs.append(("x", j, rest, None, hi))
+        else:
+            trs.append(("x", j, rest, None, lo))
+        calls[c].append(trs)
+    relay_calls = {c: [] for c in cores}
+    for p in relays:
+        A = topo.chip(p)
+        off = None
+        for a in cores:
+            if topo.chip(a) != A:
+                off = topo.mask(p, a) if off is None else off & topo.mask(p, a)
+        lo = _bits(off)
+        for q in relays[p]:
+            dsts = relays[p][q]
+            relay_calls[p].append((mem[A].index(q),
+                                   [("r", mem[A].index(q), [o], k, e) for (o, k), e in zip(dsts, _split(lo, len(dsts)))]))
+    for c in cores:
+        for trs in calls[c] + [t for _, t in relay_calls[c]]:
+            for kind, j, dsts, k, e in trs:
+                for d in dsts:
+                    add(d, ("ax%d" % j) if kind == "x" else ("rx%d" % k), len(e))
+    gcalls = {c: [] for c in cores}
+    for c in cores:
+        A = topo.chip(c)
+        others = [p for p in mem[A] if p != c]
+        on = topo.mask(c, others[0])
+        off = on
+        for a in cores:
+            if topo.chip(a) != A:
+                off &= topo.mask(c, a)
+        engs = _bits(on & ~off) + _bits(on & off)
+        for k, a in enumerate(owned[c]):
+            gi = chips.index(topo.chip(a))
+            groups = _split(engs, len(others))
+            gcalls[c].append((k, a, gi, list(zip(others, groups))))
+            for p, e in zip(others, groups):
+                add(p, "yr%d" % gi, len(e))
+    return dict(cores=cores, chips=chips, mem=mem, owned=owned, calls=calls, relay_calls=relay_calls,
+                relays=relays, gcalls=gcalls, expect=expect)
+
+
+def rank_program(g, core, T, topo):
+    rank = T.rank_of(core)
+    if rank is None:
+        return
+    P = _plan(T, topo)
+    sem = T.sem
+    chips, mem, expect = P["chips"], P["mem"], P["expect"]
+    A = topo.chip(core)
+    me = mem[A].index(core)
+    others = [p for p in mem[A] if p != core]
+
+    def xs(j, t=None):
+        if t is None:
+            return T.xall[:, j * W:(j + 1) * W]
+        return T.xall[:, j * W + t * C:j * W + (t + 1) * C]
+
+    def xr(k, t=None):
+        if t is None:
+            return T.xrem[:, k * W:(k + 1) * W]
+        return T.xrem[:, k * W + t * C:k * W + (t + 1) * C]
+
+    def yblk(r, n=1):
+        return T.ybuf[:, r * C:(r + n) * C]
+
+    def did(c):
+        rid, pid, _ = topo.addr(c)
+        return DstId(rid=rid, pnc=pid)
+
+    sent = [0]
+
+    def emit(trs):
+        lst = []
+        for kind, j, dsts, k, e in trs:
+            dst_ap = xs(j) if kind == "x" else xr(k)
+            rs = sem["ax%d" % j] if kind == "x" else sem["rx%d" % k]
+            lst.append(RemoteDMATransfer(dst_ids=[did(d) for d in dsts], dma_engine_mask=_mk(e), remote_sem=rs,
+                                         srcs=[xs(j)], dsts=[dst_ap for _ in dsts]))
+            sent[0] += len(e)
+        g.remote_dma_fused(lst, local_sem=sem.snt)
+
+    g.sync.dma_start(xs(me), T.x[:, :]).then_inc(sem.ld, 16)
+
+    g.wait_ge(sem.ld, 16)
+    for trs in P["calls"][core]:
+        emit(trs)
+    for j, trs in P["relay_calls"][core]:
+        g.wait_ge(sem["ax%d" % j], expect[(core, "ax%d" % j)])
+        emit(trs)
+    for k, a, gi, dsts in P["gcalls"][core]:
+        r = T.rank_of(a)
+        g.wait_ge(sem["gready%d" % k], 1)
+        lst = []
+        for i, (p, e) in enumerate(dsts):
+            lst.append(RemoteDMATransfer(dst_ids=[did(p)], dma_engine_mask=_mk(e), remote_sem=sem["yr%d" % gi],
+                                         srcs=[T.gsend[:, (k * NOTH + i) * C:(k * NOTH + i + 1) * C]], dsts=[yblk(r)]))
+            sent[0] += len(e)
+        g.remote_dma_fused(lst, local_sem=sem.snt)
+    g.wait_ge(sem.snt, sent[0])
+
+    te = g.tensor
+
+    def product(out, lhs, rhs, done):
+        for t in range(KT):
+            mm = te.matmul(out, lhs(t), rhs(t), start=(t == 0), stop=(t == KT - 1))
+        mm.then_inc(done, 1)
+
+    te.wait_ge(sem.ld, 16)
+    product(T.pchip[:, me * C:(me + 1) * C], lambda t: xs(me, t), lambda t: xs(me, t), sem.mchip)
+    mine = P["relays"].get(core, {})
+    needs = [q for p in P["relays"] for q in P["relays"][p]]
+    order = sorted(others, key=lambda p: 0 if p in mine else (1 if p in needs else 2))
+    for p in order:
+        j = mem[A].index(p)
+        te.wait_ge(sem["ax%d" % j], expect[(core, "ax%d" % j)])
+        product(T.pchip[:, j * C:(j + 1) * C], lambda t: xs(me, t), lambda t, j=j: xs(j, t), sem.mchip)
+    for k, a in enumerate(P["owned"][core]):
+        te.wait_ge(sem["rx%d" % k], expect[(core, "rx%d" % k)])
+        for i, p in enumerate(others):
+            j = mem[A].index(p)
+            product(T["poth%d" % k][:, i * C:(i + 1) * C], lambda t, j=j: xs(j, t), lambda t, k=k: xr(k, t),
+                    sem["moth%d" % k])
+        product(T["pmine%d" % k][:, 0:C], lambda t: xs(me, t), lambda t, k=k: xr(k, t), sem["mmine%d" % k])
+
+    ve = g.vector
+    gA = chips.index(A)
+    base = {i: min(T.rank_of(c) for c in mem[ch]) for i, ch in enumerate(chips)}
+    nloc = {i: 0 for i in range(len(chips))}
+    ve.wait_ge(sem.mchip, len(mem[A]))
+    ve.tensor_copy(yblk(base[gA], len(mem[A])), T.pchip[:, 0:len(mem[A]) * C]).then_inc(sem["yl%d" % gA], 1)
+    nloc[gA] += 1
+    for k, a in enumerate(P["owned"][core]):
+        gi = chips.index(topo.chip(a))
+        ve.wait_ge(sem["moth%d" % k], NOTH)
+        ve.tensor_copy(T.gsend[:, k * NOTH * C:(k + 1) * NOTH * C], T["poth%d" % k][:, 0:NOTH * C]).then_inc(
+            sem["gready%d" % k], 1)
+        ve.wait_ge(sem["mmine%d" % k], 1)
+        ve.tensor_copy(yblk(T.rank_of(a)), T["pmine%d" % k][:, 0:C]).then_inc(sem["yl%d" % gi], 1)
+        nloc[gi] += 1
+
+    def late(i):
+        return sum(1 for c in mem[chips[i]] if not topo.may_write(c, core))
+    rest = sorted([i for i in range(len(chips)) if i != gA], key=late)
+    for q, gs in ((g.scalar, rest[:1]), (g.sync, [gA] + rest[1:])):
+        for i in gs:
+            if nloc[i]:
+                q.wait_ge(sem["yl%d" % i], nloc[i])
+            if expect.get((core, "yr%d" % i), 0):
+                q.wait_ge(sem["yr%d" % i], expect[(core, "yr%d" % i)])
+            n = len(mem[chips[i]])
+            q.dma_start(T.y[:, base[i] * C:(base[i] + n) * C], yblk(base[i], n)).then_inc(sem["st%d" % i], 16)
+        for i in gs:
+            q.wait_ge(sem["st%d" % i], 16)

@@ -13,14 +13,16 @@ SCRATCH = {
     "pchip": ("psum", [128, 512], "float32"),
     "poth0": ("psum", [128, 512], "float32"),
     "poth1": ("psum", [128, 512], "float32"),
+    "poth2": ("psum", [128, 512], "float32"),
     "pmine0": ("psum", [128, 512], "float32"),
     "pmine1": ("psum", [128, 512], "float32"),
 }
 SEMAPHORES = (["ld", "snt", "mchip"]
               + ["ax%d" % j for j in range(4)]
               + ["rx%d" % k for k in range(NSLOT)]
-              + ["moth%d" % k for k in range(NSLOT)] + ["mmine%d" % k for k in range(NSLOT)]
-              + ["gready%d" % k for k in range(NSLOT)]
+              + ["ml%d_%d" % (k, i) for k in range(NSLOT) for i in range(NOTH)]
+              + ["gl%d_%d" % (k, i) for k in range(NSLOT) for i in range(NOTH)]
+              + ["mmine%d" % k for k in range(NSLOT)]
               + ["yl%d" % i for i in range(3)] + ["yr%d" % i for i in range(3)] + ["st%d" % i for i in range(3)])
 
 
@@ -69,6 +71,18 @@ def _plan(T, topo):
         cand.sort(key=lambda p: 0 if topo.die(p) == topo.die(a) else 1)
         return cand[0]
 
+    def engines(c):
+        on = None
+        off = None
+        for a in cores:
+            if a != c:
+                m = topo.mask(c, a)
+                if topo.chip(a) == topo.chip(c):
+                    on = m if on is None else on & m
+                else:
+                    off = m if off is None else off & m
+        return _bits(on & off), _bits(on & ~off)
+
     calls = {c: [] for c in cores}
     expect = {}
 
@@ -80,12 +94,7 @@ def _plan(T, topo):
         A = topo.chip(c)
         j = mem[A].index(c)
         others = [p for p in mem[A] if p != c]
-        on = topo.mask(c, others[0])
-        off = on
-        for a in cores:
-            if topo.chip(a) != A:
-                off &= topo.mask(c, a)
-        lo, hi = _bits(on & off), _bits(on & ~off)
+        lo, hi = engines(c)
         cross, via = [], None
         for B in chips:
             if B != A:
@@ -100,22 +109,16 @@ def _plan(T, topo):
         if via is not None:
             calls[c].append([("x", j, [via], None, hi)])
             rest = [p for p in others if p != via]
-        trs = []
         if cross:
-            for (o, k), e in zip(cross, _split(lo, len(cross))):
-                trs.append(("r", j, [o], k, e))
+            trs = [("r", j, [o], k, e) for (o, k), e in zip(cross, _split(lo, len(cross)))]
             trs.append(("x", j, rest, None, hi))
         else:
-            trs.append(("x", j, rest, None, lo))
+            trs = [("x", j, rest, None, lo)]
         calls[c].append(trs)
     relay_calls = {c: [] for c in cores}
     for p in relays:
         A = topo.chip(p)
-        off = None
-        for a in cores:
-            if topo.chip(a) != A:
-                off = topo.mask(p, a) if off is None else off & topo.mask(p, a)
-        lo = _bits(off)
+        lo, hi = engines(p)
         for q in relays[p]:
             dsts = relays[p][q]
             relay_calls[p].append((mem[A].index(q),
@@ -129,17 +132,13 @@ def _plan(T, topo):
     for c in cores:
         A = topo.chip(c)
         others = [p for p in mem[A] if p != c]
-        on = topo.mask(c, others[0])
-        off = on
-        for a in cores:
-            if topo.chip(a) != A:
-                off &= topo.mask(c, a)
-        engs = _bits(on & ~off) + _bits(on & off)
+        lo, hi = engines(c)
+        order = [p for p in others if topo.die(p) != topo.die(c)] + [p for p in others if topo.die(p) == topo.die(c)]
         for k, a in enumerate(owned[c]):
             gi = chips.index(topo.chip(a))
-            groups = _split(engs, len(others))
-            gcalls[c].append((k, a, gi, list(zip(others, groups))))
-            for p, e in zip(others, groups):
+            groups = [hi, lo, lo + hi]
+            gcalls[c].append((k, a, gi, list(zip(order, groups))))
+            for p, e in zip(order, groups):
                 add(p, "yr%d" % gi, len(e))
     return dict(cores=cores, chips=chips, mem=mem, owned=owned, calls=calls, relay_calls=relay_calls,
                 relays=relays, gcalls=gcalls, expect=expect)
@@ -155,6 +154,7 @@ def rank_program(g, core, T, topo):
     A = topo.chip(core)
     me = mem[A].index(core)
     others = [p for p in mem[A] if p != core]
+    order = [p for p, _ in P["gcalls"][core][0][3]]
 
     def xs(j, t=None):
         if t is None:
@@ -168,6 +168,9 @@ def rank_program(g, core, T, topo):
 
     def yblk(r, n=1):
         return T.ybuf[:, r * C:(r + n) * C]
+
+    def gblk(k, i):
+        return T.gsend[:, (k * NOTH + i) * C:(k * NOTH + i + 1) * C]
 
     def did(c):
         rid, pid, _ = topo.addr(c)
@@ -195,13 +198,16 @@ def rank_program(g, core, T, topo):
         emit(trs)
     for k, a, gi, dsts in P["gcalls"][core]:
         r = T.rank_of(a)
-        g.wait_ge(sem["gready%d" % k], 1)
         lst = []
         for i, (p, e) in enumerate(dsts):
             lst.append(RemoteDMATransfer(dst_ids=[did(p)], dma_engine_mask=_mk(e), remote_sem=sem["yr%d" % gi],
-                                         srcs=[T.gsend[:, (k * NOTH + i) * C:(k * NOTH + i + 1) * C]], dsts=[yblk(r)]))
+                                         srcs=[gblk(k, i)], dsts=[yblk(r)]))
             sent[0] += len(e)
-        g.remote_dma_fused(lst, local_sem=sem.snt)
+        for i in range(NOTH - 1):
+            g.wait_ge(sem["gl%d_%d" % (k, i)], 1)
+        g.remote_dma_fused(lst[:NOTH - 1], local_sem=sem.snt)
+        g.wait_ge(sem["gl%d_%d" % (k, NOTH - 1)], 1)
+        g.remote_dma_fused(lst[NOTH - 1:], local_sem=sem.snt)
     g.wait_ge(sem.snt, sent[0])
 
     te = g.tensor
@@ -211,22 +217,28 @@ def rank_program(g, core, T, topo):
             mm = te.matmul(out, lhs(t), rhs(t), start=(t == 0), stop=(t == KT - 1))
         mm.then_inc(done, 1)
 
-    te.wait_ge(sem.ld, 16)
-    product(T.pchip[:, me * C:(me + 1) * C], lambda t: xs(me, t), lambda t: xs(me, t), sem.mchip)
+    def chip_product(j):
+        product(T.pchip[:, j * C:(j + 1) * C], lambda t: xs(me, t), lambda t: xs(j, t), sem.mchip)
+
+    def my_product(k):
+        product(T["pmine%d" % k][:, 0:C], lambda t: xs(me, t), lambda t: xr(k, t), sem["mmine%d" % k])
+
     mine = P["relays"].get(core, {})
     needs = [q for p in P["relays"] for q in P["relays"][p]]
-    order = sorted(others, key=lambda p: 0 if p in mine else (1 if p in needs else 2))
-    for p in order:
+    te.wait_ge(sem.ld, 16)
+    chip_product(me)
+    for p in sorted(others, key=lambda p: 0 if p in mine else (1 if p in needs else 2)):
         j = mem[A].index(p)
         te.wait_ge(sem["ax%d" % j], expect[(core, "ax%d" % j)])
-        product(T.pchip[:, j * C:(j + 1) * C], lambda t: xs(me, t), lambda t, j=j: xs(j, t), sem.mchip)
-    for k, a in enumerate(P["owned"][core]):
+        chip_product(j)
+    for k in range(NSLOT):
         te.wait_ge(sem["rx%d" % k], expect[(core, "rx%d" % k)])
-        for i, p in enumerate(others):
+        for i, p in enumerate(order):
             j = mem[A].index(p)
-            product(T["poth%d" % k][:, i * C:(i + 1) * C], lambda t, j=j: xs(j, t), lambda t, k=k: xr(k, t),
-                    sem["moth%d" % k])
-        product(T["pmine%d" % k][:, 0:C], lambda t: xs(me, t), lambda t, k=k: xr(k, t), sem["mmine%d" % k])
+            if k:
+                te.wait_ge(sem["gl%d_%d" % (k - 1, i)], 1)
+            product(T["poth%d" % i][:, 0:C], lambda t: xs(j, t), lambda t: xr(k, t), sem["ml%d_%d" % (k, i)])
+        my_product(k)
 
     ve = g.vector
     gA = chips.index(A)
@@ -237,9 +249,9 @@ def rank_program(g, core, T, topo):
     nloc[gA] += 1
     for k, a in enumerate(P["owned"][core]):
         gi = chips.index(topo.chip(a))
-        ve.wait_ge(sem["moth%d" % k], NOTH)
-        ve.tensor_copy(T.gsend[:, k * NOTH * C:(k + 1) * NOTH * C], T["poth%d" % k][:, 0:NOTH * C]).then_inc(
-            sem["gready%d" % k], 1)
+        for i in range(NOTH):
+            ve.wait_ge(sem["ml%d_%d" % (k, i)], 1)
+            ve.tensor_copy(gblk(k, i), T["poth%d" % i][:, 0:C]).then_inc(sem["gl%d_%d" % (k, i)], 1)
         ve.wait_ge(sem["mmine%d" % k], 1)
         ve.tensor_copy(yblk(T.rank_of(a)), T["pmine%d" % k][:, 0:C]).then_inc(sem["yl%d" % gi], 1)
         nloc[gi] += 1

from concourse.bass import DstId, RemoteDMATransfer

KT, C = 4, 128
W = KT * C
NSLOT = 2
NOTH = 3

SCRATCH = {
    "xall": ("sbuf", [128, 4 * W], "bfloat16"),
    "xrem": ("sbuf", [128, NSLOT * W], "bfloat16"),
    "gsend": ("sbuf", [128, NSLOT * NOTH * C], "bfloat16"),
    "ybuf": ("sbuf", [128, 12 * C], "bfloat16"),
    "pchip": ("psum", [128, 512], "float32"),
    "poth0": ("psum", [128, 512], "float32"),
    "poth1": ("psum", [128, 512], "float32"),
    "poth2": ("psum", [128, 512], "float32"),
    "pmine0": ("psum", [128, 512], "float32"),
    "pmine1": ("psum", [128, 512], "float32"),
}
SEMAPHORES = (["ld", "snt", "mchip"]
              + ["ax%d" % j for j in range(4)]
              + ["rx%d" % k for k in range(NSLOT)]
              + ["ml%d_%d" % (k, i) for k in range(NSLOT) for i in range(NOTH)]
              + ["gl%d_%d" % (k, i) for k in range(NSLOT) for i in range(NOTH)]
              + ["mmine%d" % k for k in range(NSLOT)]
              + ["yl%d" % i for i in range(3)] + ["yr%d" % i for i in range(3)] + ["st%d" % i for i in range(3)])


def _bits(mask):
    return [i for i in range(mask.bit_length()) if (mask >> i) & 1]


def _mk(engs):
    m = 0
    for e in engs:
        m |= 1 << e
    return m


def _split(engs, n):
    per = 1
    while per * 2 * n <= len(engs):
        per *= 2
    return [engs[i * per:(i + 1) * per] for i in range(n)]


def _plan(T, topo):
    cores = list(T.cores)
    chips = []
    for c in cores:
        if topo.chip(c) not in chips:
            chips.append(topo.chip(c))
    mem = {ch: [c for c in cores if topo.chip(c) == ch] for ch in chips}

    owned = {c: [] for c in cores}
    owner = {}
    for B in chips:
        for d in sorted(set(topo.die(o) for o in mem[B])):
            R = [o for o in mem[B] if topo.die(o) == d]
            srcs = [a for a in cores if topo.chip(a) != B and topo.die(a) == d]
            srcs.sort(key=lambda a: 0 if topo.may_write(a, R[0]) else 1)
            for i, a in enumerate(srcs):
                o = R[i % len(R)]
                owner[(a, B)] = (o, len(owned[o]))
                owned[o].append(a)

    def relay(a, dst):
        if topo.may_write(a, dst):
            return None
        cand = [p for p in mem[topo.chip(a)] if p != a and topo.may_write(p, dst)]
        cand.sort(key=lambda p: 0 if topo.die(p) == topo.die(a) else 1)
        return cand[0]

    def engines(c):
        on = None
        off = None
        for a in cores:
            if a != c:
                m = topo.mask(c, a)
                if topo.chip(a) == topo.chip(c):
                    on = m if on is None else on & m
                else:
                    off = m if off is None else off & m
        return _bits(on & off), _bits(on & ~off)

    calls = {c: [] for c in cores}
    expect = {}

    def add(dst, sem, n):
        expect[(dst, sem)] = expect.get((dst, sem), 0) + n

    relays = {}
    for c in cores:
        A = topo.chip(c)
        j = mem[A].index(c)
        others = [p for p in mem[A] if p != c]
        lo, hi = engines(c)
        cross, via = [], None
        for B in chips:
            if B != A:
                o, k = owner[(c, B)]
                p = relay(c, o)
                if p is None:
                    cross.append((o, k))
                else:
                    via = p
                    relays.setdefault(p, {}).setdefault(c, []).append((o, k))
        rest = others
        if via is not None:
            calls[c].append([("x", j, [via], None, hi)])
            rest = [p for p in others if p != via]
        if cross:
            trs = [("r", j, [o], k, e) for (o, k), e in zip(cross, _split(lo, len(cross)))]
            trs.append(("x", j, rest, None, hi))
        else:
            trs = [("x", j, rest, None, lo)]
        calls[c].append(trs)
    relay_calls = {c: [] for c in cores}
    for p in relays:
        A = topo.chip(p)
        lo, hi = engines(p)
        for q in relays[p]:
            dsts = relays[p][q]
            relay_calls[p].append((mem[A].index(q),
                                   [("r", mem[A].index(q), [o], k, e) for (o, k), e in zip(dsts, _split(lo, len(dsts)))]))
    for c in cores:
        for trs in calls[c] + [t for _, t in relay_calls[c]]:
            for kind, j, dsts, k, e in trs:
                for d in dsts:
                    add(d, ("ax%d" % j) if kind == "x" else ("rx%d" % k), len(e))
    gcalls = {c: [] for c in cores}
    for c in cores:
        A = topo.chip(c)
        others = [p for p in mem[A] if p != c]
        lo, hi = engines(c)
        order = [p for p in others if topo.die(p) != topo.die(c)] + [p for p in others if topo.die(p) == topo.die(c)]
        for k, a in enumerate(owned[c]):
            gi = chips.index(topo.chip(a))
            groups = [hi, lo, lo + hi]
            gcalls[c].append((k, a, gi, list(zip(order, groups))))
            for p, e in zip(order, groups):
                add(p, "yr%d" % gi, len(e))
    return dict(cores=cores, chips=chips, mem=mem, owned=owned, calls=calls, relay_calls=relay_calls,
                relays=relays, gcalls=gcalls, expect=expect)


def rank_program(g, core, T, topo):
    rank = T.rank_of(core)
    if rank is None:
        return
    P = _plan(T, topo)
    sem = T.sem
    chips, mem, expect = P["chips"], P["mem"], P["expect"]
    A = topo.chip(core)
    me = mem[A].index(core)
    others = [p for p in mem[A] if p != core]
    order = [p for p, _ in P["gcalls"][core][0][3]]

    def xs(j, t=None):
        if t is None:
            return T.xall[:, j * W:(j + 1) * W]
        return T.xall[:, j * W + t * C:j * W + (t + 1) * C]

    def xr(k, t=None):
        if t is None:
            return T.xrem[:, k * W:(k + 1) * W]
        return T.xrem[:, k * W + t * C:k * W + (t + 1) * C]

    def yblk(r, n=1):
        return T.ybuf[:, r * C:(r + n) * C]

    def gblk(k, i):
        return T.gsend[:, (k * NOTH + i) * C:(k * NOTH + i + 1) * C]

    def did(c):
        rid, pid, _ = topo.addr(c)
        return DstId(rid=rid, pnc=pid)

    sent = [0]

    def emit(trs):
        lst = []
        for kind, j, dsts, k, e in trs:
            dst_ap = xs(j) if kind == "x" else xr(k)
            rs = sem["ax%d" % j] if kind == "x" else sem["rx%d" % k]
            lst.append(RemoteDMATransfer(dst_ids=[did(d) for d in dsts], dma_engine_mask=_mk(e), remote_sem=rs,
                                         srcs=[xs(j)], dsts=[dst_ap for _ in dsts]))
            sent[0] += len(e)
        g.remote_dma_fused(lst, local_sem=sem.snt)

    g.sync.dma_start(xs(me), T.x[:, :]).then_inc(sem.ld, 16)

    g.wait_ge(sem.ld, 16)
    for trs in P["calls"][core]:
        emit(trs)
    for j, trs in P["relay_calls"][core]:
        g.wait_ge(sem["ax%d" % j], expect[(core, "ax%d" % j)])
        emit(trs)
    for k, a, gi, dsts in P["gcalls"][core]:
        r = T.rank_of(a)
        lst = []
        for i, (p, e) in enumerate(dsts):
            lst.append(RemoteDMATransfer(dst_ids=[did(p)], dma_engine_mask=_mk(e), remote_sem=sem["yr%d" % gi],
                                         srcs=[gblk(k, i)], dsts=[yblk(r)]))
            sent[0] += len(e)
        for i in range(NOTH - 1):
            g.wait_ge(sem["gl%d_%d" % (k, i)], 1)
        g.remote_dma_fused(lst[:NOTH - 1], local_sem=sem.snt)
        g.wait_ge(sem["gl%d_%d" % (k, NOTH - 1)], 1)
        g.remote_dma_fused(lst[NOTH - 1:], local_sem=sem.snt)
    g.wait_ge(sem.snt, sent[0])

    te = g.tensor

    def product(out, lhs, rhs, done):
        for t in range(KT):
            mm = te.matmul(out, lhs(t), rhs(t), start=(t == 0), stop=(t == KT - 1))
        mm.then_inc(done, 1)

    def chip_product(j):
        product(T.pchip[:, j * C:(j + 1) * C], lambda t: xs(me, t), lambda t: xs(j, t), sem.mchip)

    def my_product(k):
        product(T["pmine%d" % k][:, 0:C], lambda t: xs(me, t), lambda t: xr(k, t), sem["mmine%d" % k])

    mine = P["relays"].get(core, {})
    needs = [q for p in P["relays"] for q in P["relays"][p]]
    te.wait_ge(sem.ld, 16)
    chip_product(me)
    for p in sorted(others, key=lambda p: 0 if p in mine else (1 if p in needs else 2)):
        j = mem[A].index(p)
        te.wait_ge(sem["ax%d" % j], expect[(core, "ax%d" % j)])
        chip_product(j)
    for k in range(NSLOT):
        te.wait_ge(sem["rx%d" % k], expect[(core, "rx%d" % k)])
        for i, p in enumerate(order):
            j = mem[A].index(p)
            if k:
                te.wait_ge(sem["gl%d_%d" % (k - 1, i)], 1)
            product(T["poth%d" % i][:, 0:C], lambda t: xs(j, t), lambda t: xr(k, t), sem["ml%d_%d" % (k, i)])
        my_product(k)

    ve = g.vector
    gA = chips.index(A)
    base = {i: min(T.rank_of(c) for c in mem[ch]) for i, ch in enumerate(chips)}
    nloc = {i: 0 for i in range(len(chips))}
    ve.wait_ge(sem.mchip, len(mem[A]))
    ve.tensor_copy(yblk(base[gA], len(mem[A])), T.pchip[:, 0:len(mem[A]) * C]).then_inc(sem["yl%d" % gA], 1)
    nloc[gA] += 1
    for k, a in enumerate(P["owned"][core]):
        gi = chips.index(topo.chip(a))
        for i in range(NOTH):
            ve.wait_ge(sem["ml%d_%d" % (k, i)], 1)
            ve.tensor_copy(gblk(k, i), T["poth%d" % i][:, 0:C]).then_inc(sem["gl%d_%d" % (k, i)], 1)
        ve.wait_ge(sem["mmine%d" % k], 1)
        ve.tensor_copy(yblk(T.rank_of(a)), T["pmine%d" % k][:, 0:C]).then_inc(sem["yl%d" % gi], 1)
        nloc[gi] += 1

    def late(i):
        return sum(1 for c in mem[chips[i]] if not topo.may_write(c, core))
    rest = sorted([i for i in range(len(chips)) if i != gA], key=late)
    for q, gs in ((g.scalar, rest[:1]), (g.sync, [gA] + rest[1:])):
        for i in gs:
            if nloc[i]:
                q.wait_ge(sem["yl%d" % i], nloc[i])
            if expect.get((core, "yr%d" % i), 0):
                q.wait_ge(sem["yr%d" % i], expect[(core, "yr%d" % i)])
            n = len(mem[chips[i]])
            q.dma_start(T.y[:, base[i] * C:(base[i] + n) * C], yblk(base[i], n)).then_inc(sem["st%d" % i], 16)
        for i in gs:
            q.wait_ge(sem["st%d" % i], 16)
